import numpy as np, ml_dtypes
CORES = [83,85,87,115,117,119]
N = 6
import mx_ref
NC, G = 128, 4
C = np.float32(0.037)
BF = ml_dtypes.bfloat16
def cut(t, i, w=512):
    return t[:, w * i:w * i + w]
def tile(rs):
    return np.stack(rs, axis=2).reshape(128, -1).astype(BF)
def layer(w, X):
    out = []
    for i in range(G):
        for t in range(len(X)):
            p = mx_ref.matmul(mx_ref.quantize(cut(w, len(X) * i + t)), X[t])
            z = p if t == 0 else z + p
        out.append(z)
    return out
def act(Z):
    return [np.maximum(z, 0) * C for z in Z]
def pick(b):
    s = np.zeros((128, 128, 4), np.float32)
    s[np.arange(128), np.arange(128), b] = 1.0
    return mx_ref.quantize(s.reshape(128, 512).astype(BF))
def setup_inputs(rng):
    def f(*shape):
        return mx_ref.flush((rng.standard_normal(shape, dtype=np.float32) * np.exp2(rng.integers(-2, 3, shape[:-1] + (1,)))).astype(BF))
    return {"x": f(N, 128, 4 * NC), "w1": f(N, 128, G * 512), "w2": f(N, 128, 512), "a": f(N, 128, G * 512), "b": f(N, 128, N * 4 * NC)}
def setup_inputs_blocks(rng):
    d = setup_inputs(rng)
    for k in ("x", "w1", "w2", "a", "b"): d[k] = mx_ref.spread(d[k], rng, 2)
    return d
def setup_inputs_wide(rng):
    d = setup_inputs(rng)
    for k in ("x", "w1", "w2", "a", "b"): d[k] = mx_ref.flush((d[k].astype(np.float32) * np.exp2(rng.integers(-6, 7, (N, 1, 1))).astype(np.float32)).astype(BF))
    return d
def setup_inputs_zeros(rng):
    d = setup_inputs(rng); v = d["x"].reshape(N, 128, -1, 4).copy()
    v[np.broadcast_to((rng.random((N, 1, v.shape[2], 1)) < 0.33), v.shape)] = 0
    d["x"] = v.reshape(d["x"].shape)
    return d
def reference(x, w1, w2, a, b):
    H = [mx_ref.quantize(tile(act(layer(w1[j], [mx_ref.quantize(x[j])])))) for j in range(N)]
    y = np.zeros((N, 128, N * NC), np.float32)
    for r in range(N):
        qw = mx_ref.quantize(w2[r])
        for j in range(N):
            y[r][:, NC * j:NC * j + NC] = mx_ref.matmul(qw, H[j])
    S = [pick(t) for t in range(4)]
    z = np.zeros((N, 128, NC, 4), np.float32)
    for c in range(N):
        for r in range(N):
            q = mx_ref.quantize(tile(act(layer(a[r], [mx_ref.quantize(cut(b[r], c, 4 * NC))]))))
            p = np.stack([mx_ref.matmul(S[t], q) for t in range(4)], axis=2)
            z[c] = p if r == 0 else z[c] + p
    return {"y": y, "z": z.reshape(N, 128, 4 * NC)}

@@ -1,0 +1,254 @@
+import numpy as np
+from concourse.bass import DstId, RemoteDMATransfer
+from concourse.mybir import dt, AluOpType, ActivationFunctionType
+
+F8, U8, BF, F32 = "float8_e4m3fn_x4", "uint8", "bfloat16", "float32"
+SCRATCH = {
+    "xb": ("sbuf", [128, 512], BF), "w1b": ("sbuf", [128, 2048], BF), "w2b": ("sbuf", [128, 512], BF),
+    "ab": ("sbuf", [128, 2048], BF), "bb": ("sbuf", [128, 3072], BF),
+    "xq": ("sbuf", [128, 128], F8), "xs": ("sbuf", [128, 128], U8),
+    "w1q": ("sbuf", [128, 512], F8), "w1s": ("sbuf", [128, 512], U8),
+    "w2q": ("sbuf", [128, 128], F8), "w2s": ("sbuf", [128, 128], U8),
+    "aq": ("sbuf", [128, 512], F8), "as_": ("sbuf", [128, 512], U8),
+    "bq": ("sbuf", [128, 768], F8), "bs": ("sbuf", [128, 768], U8),
+    "ht": ("sbuf", [128, 512], BF), "gt": ("sbuf", [128, 3072], BF),
+    "hq": ("sbuf", [128, 768], F8), "hs": ("sbuf", [128, 768], U8),
+    "goq": ("sbuf", [128, 768], F8), "gos": ("sbuf", [128, 768], U8),
+    "giq": ("sbuf", [128, 768], F8), "gis": ("sbuf", [128, 768], U8),
+    "one": ("sbuf", [128, 128], BF), "eye": ("sbuf", [128, 128], BF), "sb": ("sbuf", [128, 2048], BF),
+    "sq": ("sbuf", [128, 512], F8), "ss": ("sbuf", [128, 512], U8),
+    "ys": ("sbuf", [128, 768], F32), "zs": ("sbuf", [128, 512], F32),
+    "ps": ("psum", [128, 4096], F32),
+}
+SEMAPHORES = (["ld_x", "ld_w1a", "ld_w1b", "ld_bf", "ld_bo", "ld_w2", "ld_a0", "ld_a1", "st", "sent",
+               "ones", "eye", "szero", "scopy", "q_s", "q_x", "q_w1a", "q_w1b", "q_w2", "q_a0", "q_a1", "q_bf", "q_bo",
+               "q_h", "q_g1", "q_g2", "m_yn", "m_yf", "c_yn", "c_yf", "c_z"]
+              + ["%s%d" % (p, i) for p in ("mh", "ah", "mg1", "ag1", "mg2", "ag2", "mz") for i in range(4)]
+              + ["%s%d" % (p, j) for p in ("h", "g") for j in range(6)])
+CONST = 0.037
+
+
+def engines(mask):
+    return [e for e in range(mask.bit_length()) if mask >> e & 1]
+
+
+def as_mask(es):
+    return sum(1 << e for e in es)
+
+
+def groups(core, T, topo):
+    on = [r for r, c in enumerate(T.cores) if topo.chip(c) == topo.chip(core)]
+    off = [r for r, c in enumerate(T.cores) if topo.chip(c) != topo.chip(core)]
+    return on, off, off[on.index(T.rank_of(core))]
+
+
+def plan(core, T, topo):
+    on, off, partner = groups(core, T, topo)
+    me = T.rank_of(core)
+    peers = [r for r in on if r != me]
+    out = engines(topo.mask(core, T.cores[partner]))
+    stay = [e for e in engines(topo.mask(core, T.cores[peers[0]])) if e not in out]
+    q, h = len(out) // 4, len(out) // 2
+    codes = [out[:q], out[q:h], out[h:]]
+    scales = [out[h:h + q], out[h + q:], out[:h]]
+    order = [partner] + [r for r in off if r != partner]
+    goff = {r: (codes[k], scales[k]) for k, r in enumerate(order)}
+    s = len(stay) // 4
+    gon = {peers[0]: stay[:s], peers[1]: stay[s:2 * s]}
+    return {"out": out, "stay": stay, "goff": goff, "gon": gon, "relay": stay[2 * s:]}
+
+
+def rank_program(g, core, T, topo):
+    me = T.rank_of(core)
+    if me is None:
+        return
+    S = T.sem
+    on, off, partner = groups(core, T, topo)
+    peers = [r for r in on if r != me]
+    P = plan(core, T, topo)
+    n0, f0 = 128 * on[0], 128 * off[0]
+    W = 128 * len(on)
+    V, E, A, Y = g.vector, g.tensor, g.scalar, g.sync
+    RELU, COPY = ActivationFunctionType.Relu, ActivationFunctionType.Copy
+
+    def bank(k, n=128):
+        return T.ps[:, 512 * k:512 * k + n]
+
+    Y.dma_start(T.xb[:], T.x[:]).then_inc(S.ld_x, 16)
+    Y.dma_start(T.w1b[:, 0:1024], T.w1[:, 0:1024]).then_inc(S.ld_w1a, 16)
+    A.dma_start(T.w1b[:, 1024:2048], T.w1[:, 1024:2048]).then_inc(S.ld_w1b, 16)
+    A.dma_start(T.ab[:, 0:1024], T.a[:, 0:1024]).then_inc(S.ld_a0, 16)
+    Y.dma_start(T.bb[:, 4 * f0:4 * (f0 + W)], T.b[:, 4 * f0:4 * (f0 + W)]).then_inc(S.ld_bf, 16)
+    A.dma_start(T.ab[:, 1024:2048], T.a[:, 1024:2048]).then_inc(S.ld_a1, 16)
+    Y.dma_start(T.bb[:, 4 * n0:4 * (n0 + W)], T.b[:, 4 * n0:4 * (n0 + W)]).then_inc(S.ld_bo, 16)
+    Y.dma_start(T.w2b[:], T.w2[:]).then_inc(S.ld_w2, 16)
+
+    V.memset(T.one[:], 1.0).then_inc(S.ones, 1)
+    V.memset(T.sb[:], 0.0).then_inc(S.szero, 1)
+    g.wait_ge(S.ones, 1)
+    g.affine_select(T.eye[:], T.one[:], [[-1, 128]], AluOpType.is_equal, 0.0, 0, 1).then_inc(S.eye, 1)
+    V.wait_ge(S.szero, 1)
+    V.wait_ge(S.eye, 1)
+    for b in range(4):
+        V.tensor_copy(T.sb[:, 512 * b + b:512 * b + 512:4], T.eye[:]).then_inc(S.scopy, 1)
+    V.wait_ge(S.scopy, 4)
+    V.quantize_mx(T.sq[:], T.ss[:], T.sb[:]).then_inc(S.q_s, 1)
+
+    def steps_v(i, src, dst, m, done):
+        V.wait_ge(S["%s%d" % (m, i)], 1)
+        V.tensor_scalar(dst, src, CONST, 0.0, AluOpType.mult, AluOpType.max).then_inc(S["%s%d" % (done, i)], 1)
+
+    def steps_a(i, src, dst, m, done):
+        A.wait_ge(S["%s%d" % (m, i)], 1)
+        A.activation(dst, src, RELU, scale=CONST).then_inc(S["%s%d" % (done, i)], 1)
+
+    def quant(q, s, src, a, b, done):
+        V.quantize_mx(T[q][:, a:b], T[s][:, a:b], T[src][:, 4 * a:4 * b]).then_inc(S[done], 1)
+
+    V.wait_ge(S.ld_x, 16)
+    quant("xq", "xs", "xb", 0, 128, "q_x")
+    V.wait_ge(S.ld_w1a, 16)
+    quant("w1q", "w1s", "w1b", 0, 256, "q_w1a")
+    V.wait_ge(S.ld_w1b, 16)
+    quant("w1q", "w1s", "w1b", 256, 512, "q_w1b")
+    for i in range(4):
+        (steps_v if i % 2 else steps_a)(i, bank(i), T.ht[:, i:512:4], "mh", "ah")
+    for i in range(4):
+        V.wait_ge(S["ah%d" % i], 1)
+    V.quantize_mx(T.hq[:, 128 * me:128 * me + 128], T.hs[:, 128 * me:128 * me + 128], T.ht[:]).then_inc(S.q_h, 1)
+    V.wait_ge(S.ld_bf, 16)
+    quant("bq", "bs", "bb", f0, f0 + W, "q_bf")
+    V.wait_ge(S.ld_a0, 16)
+    quant("aq", "as_", "ab", 0, 256, "q_a0")
+    V.wait_ge(S.ld_a1, 16)
+    quant("aq", "as_", "ab", 256, 512, "q_a1")
+
+    def gtile(i, c0):
+        return T.gt[:, 4 * c0 + i:4 * (c0 + W):4]
+
+    for i in range(4):
+        if i == 3:
+            V.wait_ge(S.ld_bo, 16)
+            quant("bq", "bs", "bb", n0, n0 + W, "q_bo")
+        (steps_v if i % 2 else steps_a)(i, bank(4 + i, W), gtile(i, f0), "mg1", "ag1")
+    for i in range(4):
+        V.wait_ge(S["ag1%d" % i], 1)
+    quant("goq", "gos", "gt", f0, f0 + W, "q_g1")
+    V.wait_ge(S.ld_w2, 16)
+    quant("w2q", "w2s", "w2b", 0, 128, "q_w2")
+    for i in range(4):
+        (steps_v if i % 2 else steps_a)(i, bank(i, W), gtile(i, n0), "mg2", "ag2")
+    for i in range(4):
+        V.wait_ge(S["ag2%d" % i], 1)
+    quant("goq", "gos", "gt", n0, n0 + W, "q_g2")
+
+    E.wait_ge(S.q_x, 1)
+    for i in range(4):
+        if i % 2 == 0:
+            E.wait_ge(S.q_w1b if i else S.q_w1a, 1)
+        E.matmul_mx(bank(i), T.w1q[:, 128 * i:128 * i + 128], T.w1s[:, 128 * i:128 * i + 128],
+                    T.xq[:], T.xs[:], True, True).then_inc(S["mh%d" % i], 1)
+    E.wait_ge(S.q_bf, 1)
+    for i in range(4):
+        if i % 2 == 0:
+            E.wait_ge(S.q_a1 if i else S.q_a0, 1)
+        E.matmul_mx(bank(4 + i, W), T.aq[:, 128 * i:128 * i + 128], T.as_[:, 128 * i:128 * i + 128],
+                    T.bq[:, f0:f0 + W], T.bs[:, f0:f0 + W], True, True).then_inc(S["mg1%d" % i], 1)
+    E.wait_ge(S.q_bo, 1)
+    for i in range(4):
+        E.wait_ge(S["ah%d" % i], 1)
+        E.matmul_mx(bank(i, W), T.aq[:, 128 * i:128 * i + 128], T.as_[:, 128 * i:128 * i + 128],
+                    T.bq[:, n0:n0 + W], T.bs[:, n0:n0 + W], True, True).then_inc(S["mg2%d" % i], 1)
+
+    def h_count(r):
+        if r in on:
+            return 2 * len(P["stay"])
+        if r == partner:
+            return 2 * len(P["out"])
+        via = [k for k in peers if groups(T.cores[k], T, topo)[2] == r][0]
+        return 2 * len(plan(T.cores[via], T, topo)["relay"])
+
+    def g_count(r):
+        p = plan(T.cores[r], T, topo)
+        return 2 * len(p["gon"][me]) if r in on else len(p["goff"][me][0]) + len(p["goff"][me][1])
+
+    def y_half(k, c0, ranks, done):
+        for r in ranks:
+            E.wait_ge(S["h%d" % r], h_count(r))
+        E.wait_ge(S["ag2%d" % k], 1)
+        E.matmul_mx(bank(k, W), T.w2q[:], T.w2s[:], T.hq[:, c0:c0 + W], T.hs[:, c0:c0 + W], True, True).then_inc(S[done], 1)
+
+    def z_part(q, s, r, first, last):
+        for b in range(4):
+            if first:
+                E.wait_ge(S["ag1%d" % b], 1)
+            m = E.matmul_mx(bank(4 + b), T.sq[:, 128 * b:128 * b + 128], T.ss[:, 128 * b:128 * b + 128],
+                            T[q][:, 128 * r:128 * r + 128], T[s][:, 128 * r:128 * r + 128], first, last)
+            if last:
+                m.then_inc(S["mz%d" % b], 1)
+
+    E.wait_ge(S.q_w2, 1)
+    E.wait_ge(S.q_h, 1)
+    y_half(0, n0, peers, "m_yn")
+    E.wait_ge(S.q_s, 1)
+    E.wait_ge(S.q_g2, 1)
+    z_part("goq", "gos", me, True, False)
+    for r in peers:
+        E.wait_ge(S["g%d" % r], g_count(r))
+        z_part("giq", "gis", r, False, False)
+    y_half(1, f0, off, "m_yf")
+    for r in off:
+        E.wait_ge(S["g%d" % r], g_count(r))
+        z_part("giq", "gis", r, False, r == off[-1])
+
+    A.wait_ge(S.m_yn, 1)
+    A.activation(T.ys[:, n0:n0 + W], bank(0, W), COPY).then_inc(S.c_yn, 1)
+    V.wait_ge(S.m_yf, 1)
+    V.tensor_copy(T.ys[:, f0:f0 + W], bank(1, W)).then_inc(S.c_yf, 1)
+    for b in range(4):
+        Q = V if b % 2 else A
+        Q.wait_ge(S["mz%d" % b], 1)
+        if b % 2:
+            V.tensor_copy(T.zs[:, b:512:4], bank(4 + b)).then_inc(S.c_z, 1)
+        else:
+            A.activation(T.zs[:, b:512:4], bank(4 + b), COPY).then_inc(S.c_z, 1)
+    Y.wait_ge(S.c_yn, 1)
+    Y.dma_start(T.y[:, n0:n0 + W], T.ys[:, n0:n0 + W]).then_inc(S.st, 16)
+    Y.wait_ge(S.c_yf, 1)
+    Y.dma_start(T.y[:, f0:f0 + W], T.ys[:, f0:f0 + W]).then_inc(S.st, 16)
+    Y.wait_ge(S.c_z, 4)
+    Y.dma_start(T.z[:], T.zs[:]).then_inc(S.st, 16)
+    Y.wait_ge(S.st, 48)
+
+    def view(name, r):
+        v = T[name][:, 128 * r:128 * r + 128]
+        return v.bitcast(dt.uint8) if name[-1] == "q" else v
+
+    def to(ranks, src, sr, dst, dr, es, sem):
+        ids = []
+        for r in ranks:
+            rid, pid, _ = topo.addr(T.cores[r])
+            ids.append(DstId(rid=rid, pnc=pid))
+        return RemoteDMATransfer(dst_ids=ids, dma_engine_mask=as_mask(es), remote_sem=S[sem],
+                                 srcs=[view(src, sr)], dsts=[view(dst, dr) for r in ranks])
+
+    sent = [0]
+
+    def send(ts, count):
+        g.remote_dma_fused(ts, local_sem=S.sent)
+        sent[0] += count
+
+    g.wait_ge(S.q_h, 1)
+    for k in ("hq", "hs"):
+        send([to([partner], k, me, k, me, P["out"], "h%d" % me), to(peers, k, me, k, me, P["stay"], "h%d" % me)],
+             len(P["out"]) + len(P["stay"]))
+    g.wait_ge(S.q_g1, 1)
+    for j, (so, si) in enumerate((("goq", "giq"), ("gos", "gis"))):
+        send([to([r], so, r, si, me, P["goff"][r][j], "g%d" % me) for r in off], sum(len(P["goff"][r][j]) for r in off))
+    g.wait_ge(S.q_g2, 1)
+    g.wait_ge(S["h%d" % partner], h_count(partner))
+    for k, so, si in (("hq", "goq", "giq"), ("hs", "gos", "gis")):
+        send([to(peers, k, partner, k, partner, P["relay"], "h%d" % partner)]
+             + [to([r], so, r, si, me, P["gon"][r], "g%d" % me) for r in peers],
+             len(P["relay"]) + sum(len(P["gon"][r]) for r in peers))
+    g.wait_ge(S.sent, sent[0])

@@ -15,17 +15,28 @@ SCRATCH = {
     "hq": ("sbuf", [128, 768], F8), "hs": ("sbuf", [128, 768], U8),
     "goq": ("sbuf", [128, 768], F8), "gos": ("sbuf", [128, 768], U8),
     "giq": ("sbuf", [128, 768], F8), "gis": ("sbuf", [128, 768], U8),
+    "vq": ("sbuf", [128, 768], F8), "vs": ("sbuf", [128, 768], U8),
     "one": ("sbuf", [128, 128], BF), "eye": ("sbuf", [128, 128], BF), "sb": ("sbuf", [128, 2048], BF),
     "sq": ("sbuf", [128, 512], F8), "ss": ("sbuf", [128, 512], U8),
     "ys": ("sbuf", [128, 768], F32), "zs": ("sbuf", [128, 512], F32),
     "ps": ("psum", [128, 4096], F32),
 }
-SEMAPHORES = (["ld_x", "ld_w1a", "ld_w1b", "ld_bf", "ld_bo", "ld_w2", "ld_a0", "ld_a1", "st", "sent",
-               "ones", "eye", "szero", "scopy", "q_s", "q_x", "q_w1a", "q_w1b", "q_w2", "q_a0", "q_a1", "q_bf", "q_bo",
-               "q_h", "q_g1", "q_g2", "m_yn", "m_yf", "c_yn", "c_yf", "c_z"]
-              + ["%s%d" % (p, i) for p in ("mh", "ah", "mg1", "ag1", "mg2", "ag2", "mz") for i in range(4)]
-              + ["%s%d" % (p, j) for p in ("h", "g") for j in range(6)])
+LOADS = ("x", "w1a", "w1b", "ba", "bf", "bp", "bm", "w2", "a0", "a1")
+GR = ("h", "ga", "gb", "g2", "g3")
+SEMAPHORES = (["ld_" + k for k in LOADS] + ["q_" + k for k in LOADS] + ["q_" + k for k in GR]
+              + ["st", "sent", "ones", "eye", "szero", "scopy", "q_s", "m_yn", "m_yf", "c_yn", "c_yf", "c_z"]
+              + ["%s%s%d" % (p, k, i) for p in ("m", "a") for k in GR for i in range(4)]
+              + ["mz%d" % i for i in range(4)]
+              + ["%s%d" % (p, j) for p in ("h", "g", "v") for j in range(6)])
 CONST = 0.037
+V_ORDER = ["x", "w1a", "w1b", "h.1", "ba", "Qh", "a0", "a1", "bf", "ga.3", "Qga", "bp", "gb.3", "Qgb", "w2",
+           "g2.1", "g2.3", "Qg2", "bm", "S", "g3.1", "g3.3", "Qg3"]
+A_ORDER = ["h.0", "h.2", "h.3", "ga.0", "ga.1", "ga.2", "gb.0", "gb.1", "gb.2", "g2.0", "g2.2", "g3.0", "g3.2"]
+E_ORDER = ["h", "ga", "gb", "g2", "g3", "zm", "yn", "zp", "yf", "zd", "zv"]
+Y_LOADS = ["x", "a0", "bf", "bp", "w2"]
+A_LOADS = ["w1a", "w1b", "ba", "a1", "bm"]
+SENDS = ["h", "ga", "gb", "g2", "on"]
+STORES = [("yn", "A"), ("yf", "V"), ("z", "AVAV")]
 
 
 def engines(mask):
@@ -42,20 +53,24 @@ def groups(core, T, topo):
     return on, off, off[on.index(T.rank_of(core))]
 
 
+def hub_of(core, T, topo):
+    on = groups(core, T, topo)[0]
+    return [r for r in on if sum(topo.die(T.cores[k]) == topo.die(T.cores[r]) for k in on) == 1][0]
+
+
 def plan(core, T, topo):
     on, off, partner = groups(core, T, topo)
-    me = T.rank_of(core)
+    me, hub = T.rank_of(core), hub_of(core, T, topo)
     peers = [r for r in on if r != me]
     out = engines(topo.mask(core, T.cores[partner]))
     stay = [e for e in engines(topo.mask(core, T.cores[peers[0]])) if e not in out]
-    q, h = len(out) // 4, len(out) // 2
-    codes = [out[:q], out[q:h], out[h:]]
-    scales = [out[h:h + q], out[h + q:], out[:h]]
-    order = [partner] + [r for r in off if r != partner]
-    goff = {r: (codes[k], scales[k]) for k, r in enumerate(order)}
-    s = len(stay) // 4
-    gon = {peers[0]: stay[:s], peers[1]: stay[s:2 * s]}
-    return {"out": out, "stay": stay, "goff": goff, "gon": gon, "relay": stay[2 * s:]}
+
+    def halves(es):
+        return [es[:len(es) // 2], es[len(es) // 2:]]
+    far = [r for r in off if r != partner]
+    return {"hoff": out, "hon": stay, "ga": out if me == hub else stay, "gb": dict(zip(far, halves(out))),
+            "fwd": dict(zip(peers, halves(out))) if me == hub else {}, "g2": dict(zip(peers, halves(stay))),
+            "relay": stay if me == hub else out + stay}
 
 
 def rank_program(g, core, T, topo):
@@ -64,24 +79,37 @@ def rank_program(g, core, T, topo):
         return
     S = T.sem
     on, off, partner = groups(core, T, topo)
+    hub = hub_of(core, T, topo)
     peers = [r for r in on if r != me]
-    P = plan(core, T, topo)
+    far = [r for r in off if r != partner]
+    plans = [plan(c, T, topo) for c in T.cores]
+    partners = [groups(c, T, topo)[2] for c in T.cores]
+    P = plans[me]
     n0, f0 = 128 * on[0], 128 * off[0]
     W = 128 * len(on)
+    slot = {r: k for k, r in enumerate([partner] + far + peers + [me])}
     V, E, A, Y = g.vector, g.tensor, g.scalar, g.sync
     RELU, COPY = ActivationFunctionType.Relu, ActivationFunctionType.Copy
 
     def bank(k, n=128):
         return T.ps[:, 512 * k:512 * k + n]
 
-    Y.dma_start(T.xb[:], T.x[:]).then_inc(S.ld_x, 16)
-    Y.dma_start(T.w1b[:, 0:1024], T.w1[:, 0:1024]).then_inc(S.ld_w1a, 16)
-    A.dma_start(T.w1b[:, 1024:2048], T.w1[:, 1024:2048]).then_inc(S.ld_w1b, 16)
-    A.dma_start(T.ab[:, 0:1024], T.a[:, 0:1024]).then_inc(S.ld_a0, 16)
-    Y.dma_start(T.bb[:, 4 * f0:4 * (f0 + W)], T.b[:, 4 * f0:4 * (f0 + W)]).then_inc(S.ld_bf, 16)
-    A.dma_start(T.ab[:, 1024:2048], T.a[:, 1024:2048]).then_inc(S.ld_a1, 16)
-    Y.dma_start(T.bb[:, 4 * n0:4 * (n0 + W)], T.b[:, 4 * n0:4 * (n0 + W)]).then_inc(S.ld_bo, 16)
-    Y.dma_start(T.w2b[:], T.w2[:]).then_inc(S.ld_w2, 16)
+    def btiles(rs):
+        out = []
+        for r in rs:
+            if out and out[-1][3] + out[-1][4] == 512 * r:
+                out[-1][4] += 512
+            else:
+                out.append(["bb", 512 * slot[r], "b", 512 * r, 512])
+        return out
+
+    pieces = {"x": [["xb", 0, "x", 0, 512]], "w1a": [["w1b", 0, "w1", 0, 1024]], "w1b": [["w1b", 1024, "w1", 1024, 1024]],
+              "a0": [["ab", 0, "a", 0, 1024]], "a1": [["ab", 1024, "a", 1024, 1024]], "w2": [["w2b", 0, "w2", 0, 512]],
+              "ba": btiles([partner]), "bf": btiles(far), "bp": btiles(peers), "bm": btiles([me])}
+    for Q, order in ((Y, Y_LOADS), (A, A_LOADS)):
+        for k in order:
+            for d, dc, s, sc, n in pieces[k]:
+                Q.dma_start(T[d][:, dc:dc + n], T[s][:, sc:sc + n]).then_inc(S["ld_" + k], 16)
 
     V.memset(T.one[:], 1.0).then_inc(S.ones, 1)
     V.memset(T.sb[:], 0.0).then_inc(S.szero, 1)
@@ -91,164 +119,163 @@ def rank_program(g, core, T, topo):
     V.wait_ge(S.eye, 1)
     for b in range(4):
         V.tensor_copy(T.sb[:, 512 * b + b:512 * b + 512:4], T.eye[:]).then_inc(S.scopy, 1)
-    V.wait_ge(S.scopy, 4)
-    V.quantize_mx(T.sq[:], T.ss[:], T.sb[:]).then_inc(S.q_s, 1)
 
-    def steps_v(i, src, dst, m, done):
-        V.wait_ge(S["%s%d" % (m, i)], 1)
-        V.tensor_scalar(dst, src, CONST, 0.0, AluOpType.mult, AluOpType.max).then_inc(S["%s%d" % (done, i)], 1)
+    quants = {"x": ("xq", "xs", "xb", 0, 128), "w1a": ("w1q", "w1s", "w1b", 0, 256), "w1b": ("w1q", "w1s", "w1b", 256, 512),
+              "a0": ("aq", "as_", "ab", 0, 256), "a1": ("aq", "as_", "ab", 256, 512), "w2": ("w2q", "w2s", "w2b", 0, 128)}
+    G = {"h": ("ht", 0, 128, 0, None), "ga": ("gt", 0, 128, 4, None), "gb": ("gt", 128, 256, 0, "h"),
+         "g2": ("gt", 384, 256, 4, "ga"), "g3": ("gt", 640, 128, 0, "gb")}
+    YB, ZB = 0, 4
+    moving = {"h": "x", "ga": "ba", "gb": "bf", "g2": "bp", "g3": "bm"}
+    for k in GR[1:]:
+        c, n = G[k][1:3]
+        quants[moving[k]] = ("bq", "bs", "bb", c, c + n)
+        quants[k] = ("goq", "gos", "gt", c, c + n)
 
-    def steps_a(i, src, dst, m, done):
-        A.wait_ge(S["%s%d" % (m, i)], 1)
-        A.activation(dst, src, RELU, scale=CONST).then_inc(S["%s%d" % (done, i)], 1)
+    def step(Q, k):
+        name, i = k.split(".")
+        t, c, n, bk, _ = G[name]
+        i = int(i)
+        dst, src = T[t][:, 4 * c + i:4 * (c + n):4], bank(bk + i, n)
+        Q.wait_ge(S["m%s%d" % (name, i)], 1)
+        if Q is V:
+            V.tensor_scalar(dst, src, CONST, 0.0, AluOpType.mult, AluOpType.max).then_inc(S["a%s%d" % (name, i)], 1)
+        else:
+            A.activation(dst, src, RELU, scale=CONST).then_inc(S["a%s%d" % (name, i)], 1)
 
-    def quant(q, s, src, a, b, done):
-        V.quantize_mx(T[q][:, a:b], T[s][:, a:b], T[src][:, 4 * a:4 * b]).then_inc(S[done], 1)
-
-    V.wait_ge(S.ld_x, 16)
-    quant("xq", "xs", "xb", 0, 128, "q_x")
-    V.wait_ge(S.ld_w1a, 16)
-    quant("w1q", "w1s", "w1b", 0, 256, "q_w1a")
-    V.wait_ge(S.ld_w1b, 16)
-    quant("w1q", "w1s", "w1b", 256, 512, "q_w1b")
-    for i in range(4):
-        (steps_v if i % 2 else steps_a)(i, bank(i), T.ht[:, i:512:4], "mh", "ah")
-    for i in range(4):
-        V.wait_ge(S["ah%d" % i], 1)
-    V.quantize_mx(T.hq[:, 128 * me:128 * me + 128], T.hs[:, 128 * me:128 * me + 128], T.ht[:]).then_inc(S.q_h, 1)
-    V.wait_ge(S.ld_bf, 16)
-    quant("bq", "bs", "bb", f0, f0 + W, "q_bf")
-    V.wait_ge(S.ld_a0, 16)
-    quant("aq", "as_", "ab", 0, 256, "q_a0")
-    V.wait_ge(S.ld_a1, 16)
-    quant("aq", "as_", "ab", 256, 512, "q_a1")
-
-    def gtile(i, c0):
-        return T.gt[:, 4 * c0 + i:4 * (c0 + W):4]
-
-    for i in range(4):
-        if i == 3:
-            V.wait_ge(S.ld_bo, 16)
-            quant("bq", "bs", "bb", n0, n0 + W, "q_bo")
-        (steps_v if i % 2 else steps_a)(i, bank(4 + i, W), gtile(i, f0), "mg1", "ag1")
-    for i in range(4):
-        V.wait_ge(S["ag1%d" % i], 1)
-    quant("goq", "gos", "gt", f0, f0 + W, "q_g1")
-    V.wait_ge(S.ld_w2, 16)
-    quant("w2q", "w2s", "w2b", 0, 128, "q_w2")
-    for i in range(4):
-        (steps_v if i % 2 else steps_a)(i, bank(i, W), gtile(i, n0), "mg2", "ag2")
-    for i in range(4):
-        V.wait_ge(S["ag2%d" % i], 1)
-    quant("goq", "gos", "gt", n0, n0 + W, "q_g2")
-
-    E.wait_ge(S.q_x, 1)
-    for i in range(4):
-        if i % 2 == 0:
-            E.wait_ge(S.q_w1b if i else S.q_w1a, 1)
-        E.matmul_mx(bank(i), T.w1q[:, 128 * i:128 * i + 128], T.w1s[:, 128 * i:128 * i + 128],
-                    T.xq[:], T.xs[:], True, True).then_inc(S["mh%d" % i], 1)
-    E.wait_ge(S.q_bf, 1)
-    for i in range(4):
-        if i % 2 == 0:
-            E.wait_ge(S.q_a1 if i else S.q_a0, 1)
-        E.matmul_mx(bank(4 + i, W), T.aq[:, 128 * i:128 * i + 128], T.as_[:, 128 * i:128 * i + 128],
-                    T.bq[:, f0:f0 + W], T.bs[:, f0:f0 + W], True, True).then_inc(S["mg1%d" % i], 1)
-    E.wait_ge(S.q_bo, 1)
-    for i in range(4):
-        E.wait_ge(S["ah%d" % i], 1)
-        E.matmul_mx(bank(i, W), T.aq[:, 128 * i:128 * i + 128], T.as_[:, 128 * i:128 * i + 128],
-                    T.bq[:, n0:n0 + W], T.bs[:, n0:n0 + W], True, True).then_inc(S["mg2%d" % i], 1)
+    for k in V_ORDER:
+        if k == "S":
+            V.wait_ge(S.scopy, 4)
+            V.quantize_mx(T.sq[:], T.ss[:], T.sb[:]).then_inc(S.q_s, 1)
+        elif "." in k:
+            step(V, k)
+        elif k == "Qh":
+            for i in range(4):
+                V.wait_ge(S["ah%d" % i], 1)
+            V.quantize_mx(T.hq[:, 128 * me:128 * me + 128], T.hs[:, 128 * me:128 * me + 128], T.ht[:]).then_inc(S.q_h, 1)
+        else:
+            if k[0] == "Q":
+                k = k[1:]
+                for i in range(4):
+                    V.wait_ge(S["a%s%d" % (k, i)], 1)
+            else:
+                V.wait_ge(S["ld_" + k], 16 * len(pieces[k]))
+            q, s, src, a, b = quants[k]
+            V.quantize_mx(T[q][:, a:b], T[s][:, a:b], T[src][:, 4 * a:4 * b]).then_inc(S["q_" + k], 1)
+    for k in A_ORDER:
+        step(A, k)
 
     def h_count(r):
         if r in on:
-            return 2 * len(P["stay"])
-        if r == partner:
-            return 2 * len(P["out"])
-        via = [k for k in peers if groups(T.cores[k], T, topo)[2] == r][0]
-        return 2 * len(plan(T.cores[via], T, topo)["relay"])
+            return 2 * len(plans[r]["hon"])
+        return 2 * len(plans[r]["hoff"] if r == partner else plans[partners[r]]["relay"])
 
     def g_count(r):
-        p = plan(T.cores[r], T, topo)
-        return 2 * len(p["gon"][me]) if r in on else len(p["goff"][me][0]) + len(p["goff"][me][1])
+        if r in on:
+            return 2 * len(plans[r]["g2"][me])
+        if r != partner:
+            return 2 * len(plans[r]["gb"][me])
+        h = hub_of(T.cores[r], T, topo)
+        return 2 * len(plans[r]["ga"] if r == h else plans[h]["fwd"][r])
 
-    def y_half(k, c0, ranks, done):
-        for r in ranks:
-            E.wait_ge(S["h%d" % r], h_count(r))
-        E.wait_ge(S["ag2%d" % k], 1)
-        E.matmul_mx(bank(k, W), T.w2q[:], T.w2s[:], T.hq[:, c0:c0 + W], T.hs[:, c0:c0 + W], True, True).then_inc(S[done], 1)
-
-    def z_part(q, s, r, first, last):
-        for b in range(4):
-            if first:
-                E.wait_ge(S["ag1%d" % b], 1)
-            m = E.matmul_mx(bank(4 + b), T.sq[:, 128 * b:128 * b + 128], T.ss[:, 128 * b:128 * b + 128],
-                            T[q][:, 128 * r:128 * r + 128], T[s][:, 128 * r:128 * r + 128], first, last)
-            if last:
-                m.then_inc(S["mz%d" % b], 1)
-
-    E.wait_ge(S.q_w2, 1)
-    E.wait_ge(S.q_h, 1)
-    y_half(0, n0, peers, "m_yn")
-    E.wait_ge(S.q_s, 1)
-    E.wait_ge(S.q_g2, 1)
-    z_part("goq", "gos", me, True, False)
-    for r in peers:
-        E.wait_ge(S["g%d" % r], g_count(r))
-        z_part("giq", "gis", r, False, False)
-    y_half(1, f0, off, "m_yf")
-    for r in off:
-        E.wait_ge(S["g%d" % r], g_count(r))
-        z_part("giq", "gis", r, False, r == off[-1])
-
-    A.wait_ge(S.m_yn, 1)
-    A.activation(T.ys[:, n0:n0 + W], bank(0, W), COPY).then_inc(S.c_yn, 1)
-    V.wait_ge(S.m_yf, 1)
-    V.tensor_copy(T.ys[:, f0:f0 + W], bank(1, W)).then_inc(S.c_yf, 1)
-    for b in range(4):
-        Q = V if b % 2 else A
-        Q.wait_ge(S["mz%d" % b], 1)
-        if b % 2:
-            V.tensor_copy(T.zs[:, b:512:4], bank(4 + b)).then_inc(S.c_z, 1)
+    late = [r for r in [partner] if r != hub_of(T.cores[r], T, topo)]
+    zr = {"zm": [me], "zp": peers, "zv": late, "zd": [r for r in [partner] + far if r not in late]}
+    zall = [r for k in E_ORDER for r in zr.get(k, [])]
+    for k in E_ORDER:
+        if k in G:
+            t, c, n, bk, old = G[k]
+            wq, ws, halves = (T.w1q, T.w1s, ("w1a", "w1b")) if k == "h" else (T.aq, T.as_, ("a0", "a1"))
+            rq, rs = (T.xq[:], T.xs[:]) if k == "h" else (T.bq[:, c:c + n], T.bs[:, c:c + n])
+            E.wait_ge(S["q_" + moving[k]], 1)
+            for i in range(4):
+                if i % 2 == 0:
+                    E.wait_ge(S["q_" + halves[i // 2]], 1)
+                if old:
+                    E.wait_ge(S["a%s%d" % (old, i)], 1)
+                E.matmul_mx(bank(bk + i, n), wq[:, 128 * i:128 * i + 128], ws[:, 128 * i:128 * i + 128],
+                            rq, rs, True, True).then_inc(S["m%s%d" % (k, i)], 1)
+        elif k in ("yn", "yf"):
+            c0, ranks, i = (n0, peers, 0) if k == "yn" else (f0, off, 1)
+            E.wait_ge(S.q_w2, 1)
+            if k == "yn":
+                E.wait_ge(S.q_h, 1)
+            E.wait_ge(S["ag3%d" % i], 1)
+            for r in ranks:
+                E.wait_ge(S["h%d" % r], h_count(r))
+            E.matmul_mx(bank(YB + i, W), T.w2q[:], T.w2s[:], T.hq[:, c0:c0 + W], T.hs[:, c0:c0 + W],
+                        True, True).then_inc(S["m_" + k], 1)
         else:
-            A.activation(T.zs[:, b:512:4], bank(4 + b), COPY).then_inc(S.c_z, 1)
-    Y.wait_ge(S.c_yn, 1)
-    Y.dma_start(T.y[:, n0:n0 + W], T.ys[:, n0:n0 + W]).then_inc(S.st, 16)
-    Y.wait_ge(S.c_yf, 1)
-    Y.dma_start(T.y[:, f0:f0 + W], T.ys[:, f0:f0 + W]).then_inc(S.st, 16)
-    Y.wait_ge(S.c_z, 4)
-    Y.dma_start(T.z[:], T.zs[:]).then_inc(S.st, 16)
+            for r in zr[k]:
+                first, last = r == zall[0], r == zall[-1]
+                if first:
+                    E.wait_ge(S.q_s, 1)
+                q, s, c = ("goq", "gos", 128 * slot[me]) if r == me else ("giq", "gis", 128 * r)
+                if r == me:
+                    E.wait_ge(S.q_g3, 1)
+                else:
+                    E.wait_ge(S["g%d" % r], g_count(r))
+                for b in range(4):
+                    if first:
+                        E.wait_ge(S["ag2%d" % b], 1)
+                    m = E.matmul_mx(bank(ZB + b), T.sq[:, 128 * b:128 * b + 128], T.ss[:, 128 * b:128 * b + 128],
+                                    T[q][:, c:c + 128], T[s][:, c:c + 128], first, last)
+                    if last:
+                        m.then_inc(S["mz%d" % b], 1)
+
+    def copy(who, dst, src, m, done):
+        if who == "V":
+            V.wait_ge(S[m], 1)
+            V.tensor_copy(dst, src).then_inc(S[done], 1)
+        else:
+            A.wait_ge(S[m], 1)
+            A.activation(dst, src, COPY).then_inc(S[done], 1)
+
+    for k, who in STORES:
+        if k == "z":
+            for b in range(4):
+                copy(who[b], T.zs[:, b:512:4], bank(ZB + b), "mz%d" % b, "c_z")
+            Y.wait_ge(S.c_z, 4)
+            Y.dma_start(T.z[:], T.zs[:]).then_inc(S.st, 16)
+        else:
+            c0, i = (n0, 0) if k == "yn" else (f0, 1)
+            copy(who, T.ys[:, c0:c0 + W], bank(YB + i, W), "m_" + k, "c_" + k)
+            Y.wait_ge(S["c_" + k], 1)
+            Y.dma_start(T.y[:, c0:c0 + W], T.ys[:, c0:c0 + W]).then_inc(S.st, 16)
     Y.wait_ge(S.st, 48)
 
-    def view(name, r):
-        v = T[name][:, 128 * r:128 * r + 128]
+    def view(name, k):
+        v = T[name][:, 128 * k:128 * k + 128]
         return v.bitcast(dt.uint8) if name[-1] == "q" else v
 
-    def to(ranks, src, sr, dst, dr, es, sem):
+    def to(ranks, src, sk, dst, dk, es, sem):
         ids = []
         for r in ranks:
             rid, pid, _ = topo.addr(T.cores[r])
             ids.append(DstId(rid=rid, pnc=pid))
         return RemoteDMATransfer(dst_ids=ids, dma_engine_mask=as_mask(es), remote_sem=S[sem],
-                                 srcs=[view(src, sr)], dsts=[view(dst, dr) for r in ranks])
+                                 srcs=[view(src, sk)], dsts=[view(dst, dk) for r in ranks]), len(es)
+
+    def part(what, c):
+        if what == "h":
+            return [to([partner], "h" + c, me, "h" + c, me, P["hoff"], "h%d" % me),
+                    to(peers, "h" + c, me, "h" + c, me, P["hon"], "h%d" % me)]
+        if what == "on":
+            return ([to([partners[r]], "v" + c, r, "gi" + c, r, es, "g%d" % r) for r, es in P["fwd"].items()]
+                    + [to(peers, "h" + c, partner, "h" + c, partner, P["relay"], "h%d" % partner)])
+        if what == "ga" and me != hub:
+            return [to([hub], "go" + c, slot[partner], "v" + c, me, P["ga"], "v%d" % me)]
+        dest = {partner: P["ga"]} if what == "ga" else P[what]
+        return [to([r], "go" + c, slot[r], "gi" + c, me, es, "g%d" % me) for r, es in dest.items()]
 
     sent = [0]
-
-    def send(ts, count):
-        g.remote_dma_fused(ts, local_sem=S.sent)
-        sent[0] += count
-
-    g.wait_ge(S.q_h, 1)
-    for k in ("hq", "hs"):
-        send([to([partner], k, me, k, me, P["out"], "h%d" % me), to(peers, k, me, k, me, P["stay"], "h%d" % me)],
-             len(P["out"]) + len(P["stay"]))
-    g.wait_ge(S.q_g1, 1)
-    for j, (so, si) in enumerate((("goq", "giq"), ("gos", "gis"))):
-        send([to([r], so, r, si, me, P["goff"][r][j], "g%d" % me) for r in off], sum(len(P["goff"][r][j]) for r in off))
-    g.wait_ge(S.q_g2, 1)
-    g.wait_ge(S["h%d" % partner], h_count(partner))
-    for k, so, si in (("hq", "goq", "giq"), ("hs", "gos", "gis")):
-        send([to(peers, k, partner, k, partner, P["relay"], "h%d" % partner)]
-             + [to([r], so, r, si, me, P["gon"][r], "g%d" % me) for r in peers],
-             len(P["relay"]) + sum(len(P["gon"][r]) for r in peers))
+    for what in SENDS:
+        if what == "on":
+            g.wait_ge(S["h%d" % partner], h_count(partner))
+            for r in P["fwd"]:
+                g.wait_ge(S["v%d" % r], 2 * len(plans[r]["ga"]))
+        else:
+            g.wait_ge(S["q_" + what], 1)
+        for c in "qs":
+            ts = part(what, c)
+            g.remote_dma_fused([t for t, n in ts], local_sem=S.sent)
+            sent[0] += sum(n for t, n in ts)
     g.wait_ge(S.sent, sent[0])

import numpy as np
from concourse.bass import DstId, RemoteDMATransfer
from concourse.mybir import dt, AluOpType, ActivationFunctionType

F8, U8, BF, F32 = "float8_e4m3fn_x4", "uint8", "bfloat16", "float32"
SCRATCH = {
    "xb": ("sbuf", [128, 512], BF), "w1b": ("sbuf", [128, 2048], BF), "w2b": ("sbuf", [128, 512], BF),
    "ab": ("sbuf", [128, 2048], BF), "bb": ("sbuf", [128, 3072], BF),
    "xq": ("sbuf", [128, 128], F8), "xs": ("sbuf", [128, 128], U8),
    "w1q": ("sbuf", [128, 512], F8), "w1s": ("sbuf", [128, 512], U8),
    "w2q": ("sbuf", [128, 128], F8), "w2s": ("sbuf", [128, 128], U8),
    "aq": ("sbuf", [128, 512], F8), "as_": ("sbuf", [128, 512], U8),
    "bq": ("sbuf", [128, 768], F8), "bs": ("sbuf", [128, 768], U8),
    "ht": ("sbuf", [128, 512], BF), "gt": ("sbuf", [128, 3072], BF),
    "hq": ("sbuf", [128, 768], F8), "hs": ("sbuf", [128, 768], U8),
    "goq": ("sbuf", [128, 768], F8), "gos": ("sbuf", [128, 768], U8),
    "giq": ("sbuf", [128, 768], F8), "gis": ("sbuf", [128, 768], U8),
    "vq": ("sbuf", [128, 768], F8), "vs": ("sbuf", [128, 768], U8),
    "one": ("sbuf", [128, 128], BF), "eye": ("sbuf", [128, 128], BF), "sb": ("sbuf", [128, 2048], BF),
    "sq": ("sbuf", [128, 512], F8), "ss": ("sbuf", [128, 512], U8),
    "ys": ("sbuf", [128, 768], F32), "zs": ("sbuf", [128, 512], F32),
    "ps": ("psum", [128, 4096], F32),
}
LOADS = ("x", "w1a", "w1b", "ba", "bf", "bp", "bm", "w2", "a0", "a1")
GR = ("h", "ga", "gb", "g2", "g3")
SEMAPHORES = (["ld_" + k for k in LOADS] + ["q_" + k for k in LOADS] + ["q_" + k for k in GR]
              + ["st", "sent", "ones", "eye", "szero", "scopy", "q_s", "m_yn", "m_yf", "c_yn", "c_yf", "c_z"]
              + ["%s%s%d" % (p, k, i) for p in ("m", "a") for k in GR for i in range(4)]
              + ["mz%d" % i for i in range(4)]
              + ["%s%d" % (p, j) for p in ("h", "g", "v") for j in range(6)])
CONST = 0.037
V_ORDER = ["x", "w1a", "w1b", "h.1", "ba", "Qh", "a0", "a1", "bf", "ga.3", "Qga", "bp", "gb.3", "Qgb", "w2",
           "g2.1", "g2.3", "Qg2", "bm", "S", "g3.1", "g3.3", "Qg3"]
A_ORDER = ["h.0", "h.2", "h.3", "ga.0", "ga.1", "ga.2", "gb.0", "gb.1", "gb.2", "g2.0", "g2.2", "g3.0", "g3.2"]
E_ORDER = ["h", "ga", "gb", "g2", "g3", "zm", "yn", "zp", "yf", "zd", "zv"]
Y_LOADS = ["x", "a0", "bf", "bp", "w2"]
A_LOADS = ["w1a", "w1b", "ba", "a1", "bm"]
SENDS = ["h", "ga", "gb", "g2", "on"]
STORES = [("yn", "A"), ("yf", "V"), ("z", "AVAV")]


def engines(mask):
    return [e for e in range(mask.bit_length()) if mask >> e & 1]


def as_mask(es):
    return sum(1 << e for e in es)


def groups(core, T, topo):
    on = [r for r, c in enumerate(T.cores) if topo.chip(c) == topo.chip(core)]
    off = [r for r, c in enumerate(T.cores) if topo.chip(c) != topo.chip(core)]
    return on, off, off[on.index(T.rank_of(core))]


def hub_of(core, T, topo):
    on = groups(core, T, topo)[0]
    return [r for r in on if sum(topo.die(T.cores[k]) == topo.die(T.cores[r]) for k in on) == 1][0]


def plan(core, T, topo):
    on, off, partner = groups(core, T, topo)
    me, hub = T.rank_of(core), hub_of(core, T, topo)
    peers = [r for r in on if r != me]
    out = engines(topo.mask(core, T.cores[partner]))
    stay = [e for e in engines(topo.mask(core, T.cores[peers[0]])) if e not in out]

    def halves(es):
        return [es[:len(es) // 2], es[len(es) // 2:]]
    far = [r for r in off if r != partner]
    return {"hoff": out, "hon": stay, "ga": out if me == hub else stay, "gb": dict(zip(far, halves(out))),
            "fwd": dict(zip(peers, halves(out))) if me == hub else {}, "g2": dict(zip(peers, halves(stay))),
            "relay": stay if me == hub else out + stay}


def rank_program(g, core, T, topo):
    me = T.rank_of(core)
    if me is None:
        return
    S = T.sem
    on, off, partner = groups(core, T, topo)
    hub = hub_of(core, T, topo)
    peers = [r for r in on if r != me]
    far = [r for r in off if r != partner]
    plans = [plan(c, T, topo) for c in T.cores]
    partners = [groups(c, T, topo)[2] for c in T.cores]
    P = plans[me]
    n0, f0 = 128 * on[0], 128 * off[0]
    W = 128 * len(on)
    slot = {r: k for k, r in enumerate([partner] + far + peers + [me])}
    V, E, A, Y = g.vector, g.tensor, g.scalar, g.sync
    RELU, COPY = ActivationFunctionType.Relu, ActivationFunctionType.Copy

    def bank(k, n=128):
        return T.ps[:, 512 * k:512 * k + n]

    def btiles(rs):
        out = []
        for r in rs:
            if out and out[-1][3] + out[-1][4] == 512 * r:
                out[-1][4] += 512
            else:
                out.append(["bb", 512 * slot[r], "b", 512 * r, 512])
        return out

    pieces = {"x": [["xb", 0, "x", 0, 512]], "w1a": [["w1b", 0, "w1", 0, 1024]], "w1b": [["w1b", 1024, "w1", 1024, 1024]],
              "a0": [["ab", 0, "a", 0, 1024]], "a1": [["ab", 1024, "a", 1024, 1024]], "w2": [["w2b", 0, "w2", 0, 512]],
              "ba": btiles([partner]), "bf": btiles(far), "bp": btiles(peers), "bm": btiles([me])}
    for Q, order in ((Y, Y_LOADS), (A, A_LOADS)):
        for k in order:
            for d, dc, s, sc, n in pieces[k]:
                Q.dma_start(T[d][:, dc:dc + n], T[s][:, sc:sc + n]).then_inc(S["ld_" + k], 16)

    V.memset(T.one[:], 1.0).then_inc(S.ones, 1)
    V.memset(T.sb[:], 0.0).then_inc(S.szero, 1)
    g.wait_ge(S.ones, 1)
    g.affine_select(T.eye[:], T.one[:], [[-1, 128]], AluOpType.is_equal, 0.0, 0, 1).then_inc(S.eye, 1)
    V.wait_ge(S.szero, 1)
    V.wait_ge(S.eye, 1)
    for b in range(4):
        V.tensor_copy(T.sb[:, 512 * b + b:512 * b + 512:4], T.eye[:]).then_inc(S.scopy, 1)

    quants = {"x": ("xq", "xs", "xb", 0, 128), "w1a": ("w1q", "w1s", "w1b", 0, 256), "w1b": ("w1q", "w1s", "w1b", 256, 512),
              "a0": ("aq", "as_", "ab", 0, 256), "a1": ("aq", "as_", "ab", 256, 512), "w2": ("w2q", "w2s", "w2b", 0, 128)}
    G = {"h": ("ht", 0, 128, 0, None), "ga": ("gt", 0, 128, 4, None), "gb": ("gt", 128, 256, 0, "h"),
         "g2": ("gt", 384, 256, 4, "ga"), "g3": ("gt", 640, 128, 0, "gb")}
    YB, ZB = 0, 4
    moving = {"h": "x", "ga": "ba", "gb": "bf", "g2": "bp", "g3": "bm"}
    for k in GR[1:]:
        c, n = G[k][1:3]
        quants[moving[k]] = ("bq", "bs", "bb", c, c + n)
        quants[k] = ("goq", "gos", "gt", c, c + n)

    def step(Q, k):
        name, i = k.split(".")
        t, c, n, bk, _ = G[name]
        i = int(i)
        dst, src = T[t][:, 4 * c + i:4 * (c + n):4], bank(bk + i, n)
        Q.wait_ge(S["m%s%d" % (name, i)], 1)
        if Q is V:
            V.tensor_scalar(dst, src, CONST, 0.0, AluOpType.mult, AluOpType.max).then_inc(S["a%s%d" % (name, i)], 1)
        else:
            A.activation(dst, src, RELU, scale=CONST).then_inc(S["a%s%d" % (name, i)], 1)

    for k in V_ORDER:
        if k == "S":
            V.wait_ge(S.scopy, 4)
            V.quantize_mx(T.sq[:], T.ss[:], T.sb[:]).then_inc(S.q_s, 1)
        elif "." in k:
            step(V, k)
        elif k == "Qh":
            for i in range(4):
                V.wait_ge(S["ah%d" % i], 1)
            V.quantize_mx(T.hq[:, 128 * me:128 * me + 128], T.hs[:, 128 * me:128 * me + 128], T.ht[:]).then_inc(S.q_h, 1)
        else:
            if k[0] == "Q":
                k = k[1:]
                for i in range(4):
                    V.wait_ge(S["a%s%d" % (k, i)], 1)
            else:
                V.wait_ge(S["ld_" + k], 16 * len(pieces[k]))
            q, s, src, a, b = quants[k]
            V.quantize_mx(T[q][:, a:b], T[s][:, a:b], T[src][:, 4 * a:4 * b]).then_inc(S["q_" + k], 1)
    for k in A_ORDER:
        step(A, k)

    def h_count(r):
        if r in on:
            return 2 * len(plans[r]["hon"])
        return 2 * len(plans[r]["hoff"] if r == partner else plans[partners[r]]["relay"])

    def g_count(r):
        if r in on:
            return 2 * len(plans[r]["g2"][me])
        if r != partner:
            return 2 * len(plans[r]["gb"][me])
        h = hub_of(T.cores[r], T, topo)
        return 2 * len(plans[r]["ga"] if r == h else plans[h]["fwd"][r])

    late = [r for r in [partner] if r != hub_of(T.cores[r], T, topo)]
    zr = {"zm": [me], "zp": peers, "zv": late, "zd": [r for r in [partner] + far if r not in late]}
    zall = [r for k in E_ORDER for r in zr.get(k, [])]
    for k in E_ORDER:
        if k in G:
            t, c, n, bk, old = G[k]
            wq, ws, halves = (T.w1q, T.w1s, ("w1a", "w1b")) if k == "h" else (T.aq, T.as_, ("a0", "a1"))
            rq, rs = (T.xq[:], T.xs[:]) if k == "h" else (T.bq[:, c:c + n], T.bs[:, c:c + n])
            E.wait_ge(S["q_" + moving[k]], 1)
            for i in range(4):
                if i % 2 == 0:
                    E.wait_ge(S["q_" + halves[i // 2]], 1)
                if old:
                    E.wait_ge(S["a%s%d" % (old, i)], 1)
                E.matmul_mx(bank(bk + i, n), wq[:, 128 * i:128 * i + 128], ws[:, 128 * i:128 * i + 128],
                            rq, rs, True, True).then_inc(S["m%s%d" % (k, i)], 1)
        elif k in ("yn", "yf"):
            c0, ranks, i = (n0, peers, 0) if k == "yn" else (f0, off, 1)
            E.wait_ge(S.q_w2, 1)
            if k == "yn":
                E.wait_ge(S.q_h, 1)
            E.wait_ge(S["ag3%d" % i], 1)
            for r in ranks:
                E.wait_ge(S["h%d" % r], h_count(r))
            E.matmul_mx(bank(YB + i, W), T.w2q[:], T.w2s[:], T.hq[:, c0:c0 + W], T.hs[:, c0:c0 + W],
                        True, True).then_inc(S["m_" + k], 1)
        else:
            for r in zr[k]:
                first, last = r == zall[0], r == zall[-1]
                if first:
                    E.wait_ge(S.q_s, 1)
                q, s, c = ("goq", "gos", 128 * slot[me]) if r == me else ("giq", "gis", 128 * r)
                if r == me:
                    E.wait_ge(S.q_g3, 1)
                else:
                    E.wait_ge(S["g%d" % r], g_count(r))
                for b in range(4):
                    if first:
                        E.wait_ge(S["ag2%d" % b], 1)
                    m = E.matmul_mx(bank(ZB + b), T.sq[:, 128 * b:128 * b + 128], T.ss[:, 128 * b:128 * b + 128],
                                    T[q][:, c:c + 128], T[s][:, c:c + 128], first, last)
                    if last:
                        m.then_inc(S["mz%d" % b], 1)

    def copy(who, dst, src, m, done):
        if who == "V":
            V.wait_ge(S[m], 1)
            V.tensor_copy(dst, src).then_inc(S[done], 1)
        else:
            A.wait_ge(S[m], 1)
            A.activation(dst, src, COPY).then_inc(S[done], 1)

    for k, who in STORES:
        if k == "z":
            for b in range(4):
                copy(who[b], T.zs[:, b:512:4], bank(ZB + b), "mz%d" % b, "c_z")
            Y.wait_ge(S.c_z, 4)
            Y.dma_start(T.z[:], T.zs[:]).then_inc(S.st, 16)
        else:
            c0, i = (n0, 0) if k == "yn" else (f0, 1)
            copy(who, T.ys[:, c0:c0 + W], bank(YB + i, W), "m_" + k, "c_" + k)
            Y.wait_ge(S["c_" + k], 1)
            Y.dma_start(T.y[:, c0:c0 + W], T.ys[:, c0:c0 + W]).then_inc(S.st, 16)
    Y.wait_ge(S.st, 48)

    def view(name, k):
        v = T[name][:, 128 * k:128 * k + 128]
        return v.bitcast(dt.uint8) if name[-1] == "q" else v

    def to(ranks, src, sk, dst, dk, es, sem):
        ids = []
        for r in ranks:
            rid, pid, _ = topo.addr(T.cores[r])
            ids.append(DstId(rid=rid, pnc=pid))
        return RemoteDMATransfer(dst_ids=ids, dma_engine_mask=as_mask(es), remote_sem=S[sem],
                                 srcs=[view(src, sk)], dsts=[view(dst, dk) for r in ranks]), len(es)

    def part(what, c):
        if what == "h":
            return [to([partner], "h" + c, me, "h" + c, me, P["hoff"], "h%d" % me),
                    to(peers, "h" + c, me, "h" + c, me, P["hon"], "h%d" % me)]
        if what == "on":
            return ([to([partners[r]], "v" + c, r, "gi" + c, r, es, "g%d" % r) for r, es in P["fwd"].items()]
                    + [to(peers, "h" + c, partner, "h" + c, partner, P["relay"], "h%d" % partner)])
        if what == "ga" and me != hub:
            return [to([hub], "go" + c, slot[partner], "v" + c, me, P["ga"], "v%d" % me)]
        dest = {partner: P["ga"]} if what == "ga" else P[what]
        return [to([r], "go" + c, slot[r], "gi" + c, me, es, "g%d" % me) for r, es in dest.items()]

    sent = [0]
    for what in SENDS:
        if what == "on":
            g.wait_ge(S["h%d" % partner], h_count(partner))
            for r in P["fwd"]:
                g.wait_ge(S["v%d" % r], 2 * len(plans[r]["ga"]))
        else:
            g.wait_ge(S["q_" + what], 1)
        for c in "qs":
            ts = part(what, c)
            g.remote_dma_fused([t for t, n in ts], local_sem=S.sent)
            sent[0] += sum(n for t, n in ts)
    g.wait_ge(S.sent, sent[0])
